import numpy as np
import ml_dtypes


def mxq(x, axis, fmt="e4m3"):
    dtype, down = {"e4m3": (ml_dtypes.float8_e4m3fn, 7), "e5m2": (ml_dtypes.float8_e5m2, 14)}[fmt]
    v = np.moveaxis(np.asarray(x, np.float32).astype(ml_dtypes.bfloat16).astype(np.float64), axis, -1)
    blocks = v.reshape(v.shape[:-1] + (-1, 32))
    amax = np.abs(blocks).max(-1, keepdims=True)
    byte = np.maximum(np.where(amax > 0, np.frexp(amax)[1] - 1 + 127, 0) - down, 1)
    scale = np.exp2(byte - 127.0)
    codes = (blocks / scale).astype(np.float32).astype(dtype).astype(np.float64)
    return np.moveaxis((codes * scale).reshape(v.shape), -1, axis)


WIDE = False


def mx_kscale(k):
    if not WIDE:
        return np.ones(k)
    levels = np.array([10, -10, 5, -5, 0])
    if k % 512:
        return np.exp2(np.random.permutation(np.resize(levels, k // 32))).repeat(32)
    a = np.empty((k // 512, 16))
    for p in range(k // 512):
        a[p, :8] = np.random.permutation(np.resize(levels, 8))
        for g in range(8):
            far = levels[np.abs(levels - a[p, g]) >= 10]
            a[p, g + 8] = far[np.random.randint(len(far))]
    return np.exp2(a.ravel()).repeat(32)


def f64(x):
    return np.asarray(x).astype(np.float64)


def striped8(idx):
    return np.asarray(idx).reshape(8, -1, 16).transpose(0, 2, 1).reshape(128, -1).astype(np.uint16)


def unstriped8(offs):
    return offs.reshape(8, 16, -1).transpose(0, 2, 1).reshape(8, -1).astype(np.int64)


def pick8(x, idx, run):
    r = np.arange(len(x))
    return x[r[:, None], idx[r % (8 * run) // run]]


E2M1 = np.array([0.0, 0.5, 1.0, 1.5, 2.0, 3.0, 4.0, 6.0, -0.0, -0.5, -1.0, -1.5, -2.0, -3.0, -4.0, -6.0])


def pack_weight(w, fmt):
    k, n = w.shape
    w = f64(np.asarray(w, np.float32).astype(ml_dtypes.bfloat16)).reshape(k // 32, 32, n)
    amax = np.abs(w).max(1)
    if fmt == "e4m3":
        byte = np.frexp(amax)[1] - 1 + 127 - 7
    else:
        mant, ex = np.frexp(amax / 6.0)
        byte = np.where(mant > 0.5, ex, ex - 1) + 127
    byte = np.clip(np.where(amax > 0, byte, 1), 1, 254)
    scaled = (w * np.exp2(127.0 - byte)[:, None, :]).reshape(k, n).astype(np.float32)
    by_word = np.ascontiguousarray(scaled.reshape(k // 512, 128, 4, n).transpose(0, 1, 3, 2))
    if fmt == "e4m3":
        words = by_word.astype(ml_dtypes.float8_e4m3fn).view(np.uint8)
    else:
        c = by_word.astype(ml_dtypes.float4_e2m1fn).view(np.uint8) & 0xF
        words = (c[..., 0::2] | (c[..., 1::2] << 4)).reshape(k // 512, 128, 2 * n)
    return np.ascontiguousarray(words), np.ascontiguousarray(byte.astype(np.uint8).reshape(k // 512, 16, n))


def unpack_weight(words, scales, fmt):
    g, _, n = scales.shape
    words = np.ascontiguousarray(words).reshape(g, 128, n, -1)
    if fmt == "e4m3":
        vals = words.view(ml_dtypes.float8_e4m3fn).astype(np.float64)
    else:
        nib = np.empty((g, 128, n, 4), np.uint8)
        nib[..., 0::2] = words & 0xF
        nib[..., 1::2] = words >> 4
        vals = E2M1[nib]
    vals = vals * np.repeat(np.exp2(scales.astype(np.float64) - 127.0), 8, axis=1)[..., None]
    return vals.transpose(0, 1, 3, 2).reshape(g * 512, n)


D, T, Q, I, E = 512, 1024, 128, 256, 512


def setup_inputs():
    n = np.random.standard_normal
    idx = np.stack([np.random.permutation(T)[:I] for _ in range(8)])
    fd = mx_kscale(D)
    ft = mx_kscale(T)
    keysp = pack_weight(n((D, T)) / fd[:, None], "e4m3")
    return {
        "query": (n((D, Q)) * 0.3 / np.sqrt(D) * fd[:, None]).astype(np.float32),
        "keys_words": keysp[0],
        "keys_scales": keysp[1],
        "fac": (np.random.uniform(16.0, 64.0, (1, T)) * ft).astype(np.float32),
        "vals": (n((T, E)) / ft[:, None]).astype(np.float32),
        "offs": striped8(idx),
    }


def reference(query, keys_words, keys_scales, fac, vals, offs):
    idx = unstriped8(offs)
    keysu = unpack_weight(keys_words, keys_scales, "e4m3")
    queryq = mxq(f64(query), 0, "e4m3")
    a = queryq.T @ keysu
    m1 = np.max(a, axis=1, keepdims=True)
    p = np.exp(a - m1)
    pk = np.exp(pick8(a, idx, 16) - m1)
    pf = np.zeros((Q, T))
    pf[np.arange(Q)[:, None], idx[np.arange(Q) % 128 // 16]] = pk
    z = np.sum(p, axis=1, keepdims=True)
    z2 = z - np.sum(pk, axis=1, keepdims=True)
    w = (p / z - (p - pf) / z2) * f64(fac)
    wt = w.T
    wtq = mxq(wt, 0, "e4m3")
    valsq = mxq(f64(vals), 0, "e4m3")
    o = wtq.T @ valsq
    return o

@@ -1,0 +1,237 @@
+from contextlib import ExitStack
+
+import concourse.mybir as mybir
+from concourse.masks import make_identity
+
+D, T, Q, I, E = 512, 1024, 128, 256, 512
+FLOPS = 2 * Q * D * T + 2 * Q * T * E
+
+F32 = mybir.dt.float32
+BF16 = mybir.dt.bfloat16
+I32 = mybir.dt.int32
+U32 = mybir.dt.uint32
+U16 = mybir.dt.uint16
+U8 = mybir.dt.uint8
+FP8X4 = mybir.dt.float8_e4m3fn_x4
+ALU = mybir.AluOpType
+ACT = mybir.ActivationFunctionType
+
+P = 128
+PACK = 4
+K_PASS = P * PACK
+PASSES = T // K_PASS
+BANK = 512
+E_HALF = E // 2
+
+
+def tile_attend_knockout_heads_kernel(tc, query, keys_words, keys_scales, fac, vals, offs, out):
+    nc = tc.nc
+    with ExitStack() as ctx:
+        sb = ctx.enter_context(tc.tile_pool(name="sb", bufs=1))
+        ps = ctx.enter_context(tc.psum_pool(name="ps", bufs=1))
+
+        def tile(name, shape, dtype, tag=""):
+            return sb.tile(shape, dtype, name=name, tag=tag, align_bytes=64)
+
+        k_scales = tile("k_scales", [P, T], U8)
+        nc.vector.memset(k_scales[:].bitcast(U32), 0)
+        q_raw = tile("q_raw", [P, PACK, Q], F32)
+        nc.sync.dma_start(out=q_raw[:], in_=query.rearrange("(p j) q -> p j q", j=PACK))
+        for quad in range(4):
+            nc.scalar.dma_start(
+                out=k_scales[32 * quad : 32 * quad + 4, :].bitcast(I32),
+                in_=keys_scales[0][4 * quad : 4 * quad + 4, :].bitcast(I32),
+            )
+        k_bytes = keys_words[0].rearrange("p n t -> p (n t)")
+        k_words = []
+        for h in range(2):
+            kw = tile(f"k_words{h}", [P, BANK], U32)
+            nc.sync.dma_start(out=kw[:].bitcast(I32), in_=k_bytes[:, h * BANK * PACK : (h + 1) * BANK * PACK].bitcast(I32))
+            k_words.append(kw)
+        offsets = sb.tile([P, I // 16], U16, name="offsets")
+        nc.sync.dma_start(offsets[:], offs)
+        fac_sb = tile("fac_sb", [P, PASSES, PACK], F32)
+        nc.gpsimd.dma_start(out=fac_sb[:], in_=fac[0].rearrange("(g p r) -> p g r", g=PASSES, r=PACK))
+        v_raw = {}
+        for g in range(PASSES):
+            rows = vals[g * K_PASS : (g + 1) * K_PASS, :].rearrange("(p j) e -> p j e", j=PACK)
+            for h in range(2):
+                vr = tile(f"v_raw{g}{h}", [P, PACK, E_HALF], F32)
+                nc.sync.dma_start(out=vr[:], in_=rows[:, :, h * E_HALF : (h + 1) * E_HALF])
+                v_raw[g, h] = vr
+
+        ident = tile("ident", [P, P], F32)
+        make_identity(nc, ident[:])
+        pf = tile("pf", [P, T], F32)
+        nc.vector.memset(pf[:], 0.0)
+        warm = tile("warm", [P, 1], F32)
+        nc.vector.memset(warm[:], 0.0)
+        warm_out = tile("warm_out", [P, 1], F32)
+        nc.scalar.activation(warm_out[:], warm[:], ACT.Exp)
+
+        q_bf = tile("q_bf", [P, Q, PACK], BF16)
+        nc.vector.tensor_copy(
+            out=q_bf[:].rearrange("p (c i) t -> p c t i", i=4),
+            in_=q_raw[:].rearrange("p t (c i) -> p c t i", i=4),
+        )
+        q_codes = tile("q_codes", [P, Q], U32)
+        q_scales = tile("q_scales", [P, Q], U8)
+        nc.vector.quantize_mx(out=q_codes[:].bitcast(FP8X4), scales=q_scales[:], in_=q_bf[:].rearrange("p q j -> p (q j)"))
+
+
+        a_sb = tile("a_sb", [P, T], F32)
+        row_max = []
+        for h in range(2):
+            a_ps = ps.tile([P, BANK], F32, name=f"a_ps{h}", tag=f"ab{h}")
+            nc.tensor.matmul_mx(
+                out=a_ps[:],
+                lhsT=q_codes[:].bitcast(FP8X4),
+                lhsT_scale=q_scales[:],
+                rhs=k_words[h][:].bitcast(FP8X4),
+                rhs_scale=k_scales[:, h * BANK : (h + 1) * BANK],
+                start=True,
+                stop=True,
+            )
+            m = tile(f"row_max{h}", [P, 1], F32)
+            nc.vector.tensor_scalar(
+                out=a_sb[:, h * BANK : (h + 1) * BANK],
+                in0=a_ps[:],
+                scalar1=1.0,
+                scalar2=row_max[-1][:] if row_max else None,
+                op0=ALU.mult,
+                op1=ALU.max,
+                accum_out=m[:],
+            )
+            row_max.append(m)
+        neg_max = tile("neg_max", [P, 1], F32)
+        nc.vector.tensor_scalar_mul(neg_max[:], row_max[-1][:], -1.0)
+
+
+        v_bf = {(g, h): tile(f"v_bf{g}{h}", [P, E_HALF, PACK], BF16) for g in range(PASSES) for h in range(2)}
+        v_codes = [tile(f"v_codes{g}", [P, E], U32) for g in range(PASSES)]
+        v_scales = [tile(f"v_scales{g}", [P, E], U8) for g in range(PASSES)]
+
+        def cast_values(engine, g, h, c0, c1):
+            cols = slice(c0, c1)
+            dst, src = v_bf[g, h][:, cols, :], v_raw[g, h][:, :, cols]
+            if engine == "gpsimd":
+                nc.gpsimd.tensor_scalar(out=dst, in0=src.rearrange("p t c -> p c t"), scalar1=1.0, scalar2=0.0, op0=ALU.mult, op1=ALU.add)
+                return
+            dst = dst.rearrange("p (c i) t -> p c t i", i=4)
+            src = src.rearrange("p t (c i) -> p c t i", i=4)
+            if engine == "scalar":
+                nc.scalar.copy(out=dst, in_=src)
+            else:
+                nc.vector.tensor_copy(out=dst, in_=src)
+
+        def quantize_values(g, h):
+            cols = slice(h * E_HALF, (h + 1) * E_HALF)
+            nc.vector.quantize_mx(
+                out=v_codes[g][:, cols].bitcast(FP8X4),
+                scales=v_scales[g][:, cols],
+                in_=v_bf[g, h][:].rearrange("p e j -> p (e j)"),
+            )
+
+        cast_values("scalar", 0, 0, 0, 128)
+        cast_values("scalar", 0, 0, 128, 256)
+        cast_values("scalar", 0, 1, 0, 128)
+
+        a_listed = tile("a_listed", [P, I], F32)
+        nc.vector.tensor_copy(a_listed[:], a_sb[:].indirect(offsets[:]))
+        pk = tile("pk", [P, I], F32)
+        sum_k = tile("sum_k", [P, 1], F32)
+        nc.scalar.activation(pk[:], a_listed[:], ACT.Exp, bias=neg_max[:], accum_out=sum_k[:])
+
+        quantize_values(0, 0)
+        nc.vector.tensor_copy(pf[:].indirect(offsets[:]), pk[:])
+        p = tile("p", [P, T], F32)
+        z = tile("z", [P, 1], F32)
+        nc.scalar.activation(p[:], a_sb[:], ACT.Exp, bias=neg_max[:], accum_out=z[:])
+        inv_z = tile("inv_z", [P, 1], F32)
+        nc.vector.reciprocal(inv_z[:], z[:])
+        neg_z2 = tile("neg_z2", [P, 1], F32)
+        nc.vector.tensor_sub(neg_z2[:], sum_k[:], z[:])
+        share = tile("share", [P, 1], F32)
+        nc.vector.tensor_mul(share[:], sum_k[:], inv_z[:])
+        neg_inv_z2 = tile("neg_inv_z2", [P, 1], F32)
+        nc.vector.reciprocal(neg_inv_z2[:], neg_z2[:])
+
+        cast_values("scalar", 0, 1, 128, 256)
+        cast_values("scalar", 1, 0, 0, 128)
+        cast_values("scalar", 1, 0, 128, 256)
+        cast_values("scalar", 1, 1, 0, 128)
+
+        fac_ps = []
+        for g in range(PASSES):
+            f = ps.tile([P, PACK, P], F32, name=f"fac_ps{g}", tag=f"ab{g}")
+            for r in range(PACK):
+                nc.tensor.transpose(f[:, r, :], fac_sb[:, g, r : r + 1].to_broadcast([P, P]), ident[:])
+            fac_ps.append(f)
+
+        u = tile("u", [P, T], F32)
+        for g in range(PASSES):
+            cols = slice(g * K_PASS, (g + 1) * K_PASS)
+            nc.vector.scalar_tensor_tensor(out=u[:, cols], in0=p[:, cols], scalar=share[:], in1=pf[:, cols], op0=ALU.mult, op1=ALU.subtract)
+        w_bf = []
+        for g in range(PASSES):
+            cols = slice(g * K_PASS, (g + 1) * K_PASS)
+            w = tile(f"w_bf{g}", [P, K_PASS], BF16)
+            nc.vector.scalar_tensor_tensor(
+                out=w[:].rearrange("q (k r) -> q k r", r=PACK),
+                in0=u[:, cols].rearrange("q (k r) -> q k r", r=PACK),
+                scalar=neg_inv_z2[:],
+                in1=fac_ps[g][:].rearrange("q r k -> q k r"),
+                op0=ALU.mult,
+                op1=ALU.mult,
+            )
+            w_bf.append(w)
+
+
+        wt_bf = []
+
+        def turn(g):
+            words = w_bf[g][:].bitcast(F32)
+            turned = ps.tile([P, 2, Q], F32, name=f"turned{g}")
+            for s in range(2):
+                nc.tensor.transpose(turned[:, s, :], words[:, s : 2 * P : 2], ident[:])
+            wt = tile(f"wt_bf{g}", [P, Q * PACK], BF16)
+            nc.scalar.copy(out=wt[:].bitcast(F32).rearrange("p (q s) -> p q s", s=2), in_=turned[:].rearrange("p s q -> p q s"))
+            wt_bf.append(wt)
+
+        w_codes = [tile(f"w_codes{g}", [P, Q], U32) for g in range(PASSES)]
+        w_scales = [tile(f"w_scales{g}", [P, Q], U8) for g in range(PASSES)]
+
+        def quantize_weights(g):
+            nc.vector.quantize_mx(out=w_codes[g][:].bitcast(FP8X4), scales=w_scales[g][:], in_=wt_bf[g][:])
+
+        turn(0)
+        turn(1)
+        quantize_values(0, 1)
+        cast_values("vector", 1, 1, 128, 256)
+        quantize_weights(0)
+        quantize_values(1, 0)
+        quantize_values(1, 1)
+        quantize_weights(1)
+
+        o_ps = [ps.tile([P, E_HALF], F32, name=f"o_ps{h}") for h in range(2)]
+        for g in range(PASSES):
+            for h in range(2):
+                cols = slice(h * E_HALF, (h + 1) * E_HALF)
+                nc.tensor.matmul_mx(
+                    out=o_ps[h][:],
+                    lhsT=w_codes[g][:].bitcast(FP8X4),
+                    lhsT_scale=w_scales[g][:],
+                    rhs=v_codes[g][:, cols].bitcast(FP8X4),
+                    rhs_scale=v_scales[g][:, cols],
+                    start=(g == 0),
+                    stop=(g == PASSES - 1),
+                )
+        for h in range(2):
+            cols = slice(h * E_HALF, (h + 1) * E_HALF)
+            o_sb = tile(f"o_sb{h}", [P, E_HALF], F32)
+            if h == 0:
+                nc.vector.tensor_copy(out=o_sb[:], in_=o_ps[h][:])
+                nc.sync.dma_start(out=out[:, cols], in_=o_sb[:])
+            else:
+                nc.scalar.copy(out=o_sb[:], in_=o_ps[h][:])
+                nc.scalar.dma_start(out=out[:, cols], in_=o_sb[:])

@@ -33,32 +33,41 @@ def tile_attend_knockout_heads_kernel(tc, query, keys_words, keys_scales, fac, v
         def tile(name, shape, dtype, tag=""):
             return sb.tile(shape, dtype, name=name, tag=tag, align_bytes=64)
 
-        k_scales = tile("k_scales", [P, T], U8)
-        nc.vector.memset(k_scales[:].bitcast(U32), 0)
+        k_scales = tile("k_scales", [P, BANK], U8)
+        nc.gpsimd.memset(k_scales[:].bitcast(U32), 0)
         q_raw = tile("q_raw", [P, PACK, Q], F32)
         nc.sync.dma_start(out=q_raw[:], in_=query.rearrange("(p j) q -> p j q", j=PACK))
         for quad in range(4):
-            nc.scalar.dma_start(
-                out=k_scales[32 * quad : 32 * quad + 4, :].bitcast(I32),
-                in_=keys_scales[0][4 * quad : 4 * quad + 4, :].bitcast(I32),
+            nc.sync.dma_start(
+                out=k_scales[32 * quad : 32 * quad + 8, :].bitcast(I32),
+                in_=keys_scales[0][4 * quad : 4 * quad + 4, :].bitcast(I32).rearrange("r (h c) -> h r c", h=2),
             )
         k_bytes = keys_words[0].rearrange("p n t -> p (n t)")
+        rows = [vals[g * K_PASS : (g + 1) * K_PASS, :].rearrange("(p j) e -> p j e", j=PACK) for g in range(PASSES)]
+        v_raw = {}
+
+        def load_values(g, c0, c1):
+            vr = tile(f"v_raw{g}_{c0}", [P, PACK, c1 - c0], F32)
+            nc.sync.dma_start(out=vr[:], in_=rows[g][:, :, c0:c1])
+            for c in range(c0, c1, P):
+                v_raw[g, c] = vr[:, :, c - c0 : c - c0 + P]
+
         k_words = []
-        for h in range(2):
+
+        def load_keys(h):
             kw = tile(f"k_words{h}", [P, BANK], U32)
             nc.sync.dma_start(out=kw[:].bitcast(I32), in_=k_bytes[:, h * BANK * PACK : (h + 1) * BANK * PACK].bitcast(I32))
             k_words.append(kw)
+
         offsets = sb.tile([P, I // 16], U16, name="offsets")
+        load_keys(0)
+        load_keys(1)
+        load_values(0, 0, 256)
         nc.sync.dma_start(offsets[:], offs)
+        load_values(0, 256, 512)
+        load_values(1, 0, 512)
         fac_sb = tile("fac_sb", [P, PASSES, PACK], F32)
         nc.gpsimd.dma_start(out=fac_sb[:], in_=fac[0].rearrange("(g p r) -> p g r", g=PASSES, r=PACK))
-        v_raw = {}
-        for g in range(PASSES):
-            rows = vals[g * K_PASS : (g + 1) * K_PASS, :].rearrange("(p j) e -> p j e", j=PACK)
-            for h in range(2):
-                vr = tile(f"v_raw{g}{h}", [P, PACK, E_HALF], F32)
-                nc.sync.dma_start(out=vr[:], in_=rows[:, :, h * E_HALF : (h + 1) * E_HALF])
-                v_raw[g, h] = vr
 
         ident = tile("ident", [P, P], F32)
         make_identity(nc, ident[:])
@@ -69,14 +78,17 @@ def tile_attend_knockout_heads_kernel(tc, query, keys_words, keys_scales, fac, v
         warm_out = tile("warm_out", [P, 1], F32)
         nc.scalar.activation(warm_out[:], warm[:], ACT.Exp)
 
-        q_bf = tile("q_bf", [P, Q, PACK], BF16)
-        nc.vector.tensor_copy(
-            out=q_bf[:].rearrange("p (c i) t -> p c t i", i=4),
-            in_=q_raw[:].rearrange("p t (c i) -> p c t i", i=4),
-        )
+        q_bf = [tile(f"q_bf{h}", [P, Q // 2, PACK], BF16) for h in range(2)]
         q_codes = tile("q_codes", [P, Q], U32)
         q_scales = tile("q_scales", [P, Q], U8)
-        nc.vector.quantize_mx(out=q_codes[:].bitcast(FP8X4), scales=q_scales[:], in_=q_bf[:].rearrange("p q j -> p (q j)"))
+        for h in range(2):
+            nc.vector.tensor_copy(
+                out=q_bf[h][:].rearrange("p (c i) t -> p c t i", i=4),
+                in_=q_raw[:, :, h * 64 : (h + 1) * 64].rearrange("p t (c i) -> p c t i", i=4),
+            )
+        for h in range(2):
+            cols = slice(h * 64, (h + 1) * 64)
+            nc.vector.quantize_mx(out=q_codes[:, cols].bitcast(FP8X4), scales=q_scales[:, cols], in_=q_bf[h][:].rearrange("p q j -> p (q j)"))
 
 
         a_sb = tile("a_sb", [P, T], F32)
@@ -88,7 +100,7 @@ def tile_attend_knockout_heads_kernel(tc, query, keys_words, keys_scales, fac, v
                 lhsT=q_codes[:].bitcast(FP8X4),
                 lhsT_scale=q_scales[:],
                 rhs=k_words[h][:].bitcast(FP8X4),
-                rhs_scale=k_scales[:, h * BANK : (h + 1) * BANK],
+                rhs_scale=k_scales[4 * h :, :],
                 start=True,
                 stop=True,
             )
@@ -107,13 +119,12 @@ def tile_attend_knockout_heads_kernel(tc, query, keys_words, keys_scales, fac, v
         nc.vector.tensor_scalar_mul(neg_max[:], row_max[-1][:], -1.0)
 
 
-        v_bf = {(g, h): tile(f"v_bf{g}{h}", [P, E_HALF, PACK], BF16) for g in range(PASSES) for h in range(2)}
-        v_codes = [tile(f"v_codes{g}", [P, E], U32) for g in range(PASSES)]
-        v_scales = [tile(f"v_scales{g}", [P, E], U8) for g in range(PASSES)]
+        v_bf = {(g, h): tile(f"v_bf{g}{h}", [P, E_HALF, PACK], BF16) for g, h in ((0, 0), (1, 0), (1, 1))}
+        v_codes, v_scales = {}, {}
 
         def cast_values(engine, g, h, c0, c1):
             cols = slice(c0, c1)
-            dst, src = v_bf[g, h][:, cols, :], v_raw[g, h][:, :, cols]
+            dst, src = v_bf[g, h][:, cols, :], v_raw[g, h * E_HALF + c0]
             if engine == "gpsimd":
                 nc.gpsimd.tensor_scalar(out=dst, in0=src.rearrange("p t c -> p c t"), scalar1=1.0, scalar2=0.0, op0=ALU.mult, op1=ALU.add)
                 return
@@ -124,42 +135,43 @@ def tile_attend_knockout_heads_kernel(tc, query, keys_words, keys_scales, fac, v
             else:
                 nc.vector.tensor_copy(out=dst, in_=src)
 
-        def quantize_values(g, h):
-            cols = slice(h * E_HALF, (h + 1) * E_HALF)
+        def quantize_values(g, h, tag=""):
+            v_codes[g, h] = tile(f"v_codes{g}{h}", [P, E_HALF], U32, tag=tag)
+            v_scales[g, h] = tile(f"v_scales{g}{h}", [P, E_HALF], U8)
             nc.vector.quantize_mx(
-                out=v_codes[g][:, cols].bitcast(FP8X4),
-                scales=v_scales[g][:, cols],
+                out=v_codes[g, h][:].bitcast(FP8X4),
+                scales=v_scales[g, h][:],
                 in_=v_bf[g, h][:].rearrange("p e j -> p (e j)"),
             )
 
         cast_values("scalar", 0, 0, 0, 128)
         cast_values("scalar", 0, 0, 128, 256)
-        cast_values("scalar", 0, 1, 0, 128)
 
-        a_listed = tile("a_listed", [P, I], F32)
+        a_listed = tile("a_listed", [P, I], F32, tag="listed")
         nc.vector.tensor_copy(a_listed[:], a_sb[:].indirect(offsets[:]))
+        p = tile("p", [P, T], F32, tag="p")
         pk = tile("pk", [P, I], F32)
         sum_k = tile("sum_k", [P, 1], F32)
         nc.scalar.activation(pk[:], a_listed[:], ACT.Exp, bias=neg_max[:], accum_out=sum_k[:])
 
         quantize_values(0, 0)
+        v_bf[0, 1] = tile("v_bf01", [P, E_HALF, PACK], BF16, tag="listed")
         nc.vector.tensor_copy(pf[:].indirect(offsets[:]), pk[:])
-        p = tile("p", [P, T], F32)
         z = tile("z", [P, 1], F32)
         nc.scalar.activation(p[:], a_sb[:], ACT.Exp, bias=neg_max[:], accum_out=z[:])
+        for g, h in ((0, 1), (1, 0), (1, 1)):
+            cast_values("scalar", g, h, 0, 128)
+            cast_values("scalar", g, h, 128, 256)
         inv_z = tile("inv_z", [P, 1], F32)
         nc.vector.reciprocal(inv_z[:], z[:])
         neg_z2 = tile("neg_z2", [P, 1], F32)
         nc.vector.tensor_sub(neg_z2[:], sum_k[:], z[:])
+
         share = tile("share", [P, 1], F32)
         nc.vector.tensor_mul(share[:], sum_k[:], inv_z[:])
         neg_inv_z2 = tile("neg_inv_z2", [P, 1], F32)
         nc.vector.reciprocal(neg_inv_z2[:], neg_z2[:])
 
-        cast_values("scalar", 0, 1, 128, 256)
-        cast_values("scalar", 1, 0, 0, 128)
-        cast_values("scalar", 1, 0, 128, 256)
-        cast_values("scalar", 1, 1, 0, 128)
 
         fac_ps = []
         for g in range(PASSES):
@@ -168,17 +180,17 @@ def tile_attend_knockout_heads_kernel(tc, query, keys_words, keys_scales, fac, v
                 nc.tensor.transpose(f[:, r, :], fac_sb[:, g, r : r + 1].to_broadcast([P, P]), ident[:])
             fac_ps.append(f)
 
-        u = tile("u", [P, T], F32)
+        u = [tile(f"u{g}", [P, K_PASS], F32, tag=f"u{g}") for g in range(PASSES)]
         for g in range(PASSES):
             cols = slice(g * K_PASS, (g + 1) * K_PASS)
-            nc.vector.scalar_tensor_tensor(out=u[:, cols], in0=p[:, cols], scalar=share[:], in1=pf[:, cols], op0=ALU.mult, op1=ALU.subtract)
+            nc.vector.scalar_tensor_tensor(out=u[g][:], in0=p[:, cols], scalar=share[:], in1=pf[:, cols], op0=ALU.mult, op1=ALU.subtract)
         w_bf = []
         for g in range(PASSES):
             cols = slice(g * K_PASS, (g + 1) * K_PASS)
             w = tile(f"w_bf{g}", [P, K_PASS], BF16)
             nc.vector.scalar_tensor_tensor(
                 out=w[:].rearrange("q (k r) -> q k r", r=PACK),
-                in0=u[:, cols].rearrange("q (k r) -> q k r", r=PACK),
+                in0=u[g][:].rearrange("q (k r) -> q k r", r=PACK),
                 scalar=neg_inv_z2[:],
                 in1=fac_ps[g][:].rearrange("q r k -> q k r"),
                 op0=ALU.mult,
@@ -206,10 +218,9 @@ def tile_attend_knockout_heads_kernel(tc, query, keys_words, keys_scales, fac, v
 
         turn(0)
         turn(1)
-        quantize_values(0, 1)
-        cast_values("vector", 1, 1, 128, 256)
+        quantize_values(0, 1, tag="p")
+        quantize_values(1, 0, tag="u0")
         quantize_weights(0)
-        quantize_values(1, 0)
         quantize_values(1, 1)
         quantize_weights(1)
 
@@ -221,8 +232,8 @@ def tile_attend_knockout_heads_kernel(tc, query, keys_words, keys_scales, fac, v
                     out=o_ps[h][:],
                     lhsT=w_codes[g][:].bitcast(FP8X4),
                     lhsT_scale=w_scales[g][:],
-                    rhs=v_codes[g][:, cols].bitcast(FP8X4),
-                    rhs_scale=v_scales[g][:, cols],
+                    rhs=v_codes[g, h][:].bitcast(FP8X4),
+                    rhs_scale=v_scales[g, h][:],
                     start=(g == 0),
                     stop=(g == PASSES - 1),
                 )

@@ -92,34 +92,32 @@ def tile_attend_knockout_heads_kernel(tc, query, keys_words, keys_scales, fac, v
 
 
         a_sb = tile("a_sb", [P, T], F32)
-        row_max = []
-        for h in range(2):
-            a_ps = ps.tile([P, BANK], F32, name=f"a_ps{h}", tag=f"ab{h}")
+        piece_max = tile("piece_max", [P, 3], F32)
+        for n, (h, c0, c1) in enumerate(((0, 0, 256), (0, 256, 512), (1, 0, 512))):
+            a_ps = ps.tile([P, c1 - c0], F32, name=f"a_ps{h}_{c0}", tag=f"ab{h}" if c1 == BANK else "a_first")
             nc.tensor.matmul_mx(
                 out=a_ps[:],
                 lhsT=q_codes[:].bitcast(FP8X4),
                 lhsT_scale=q_scales[:],
-                rhs=k_words[h][:].bitcast(FP8X4),
-                rhs_scale=k_scales[4 * h :, :],
+                rhs=k_words[h][:, c0:c1].bitcast(FP8X4),
+                rhs_scale=k_scales[4 * h :, c0:c1],
                 start=True,
                 stop=True,
             )
-            m = tile(f"row_max{h}", [P, 1], F32)
             nc.vector.tensor_scalar(
-                out=a_sb[:, h * BANK : (h + 1) * BANK],
+                out=a_sb[:, h * BANK + c0 : h * BANK + c1],
                 in0=a_ps[:],
                 scalar1=1.0,
-                scalar2=row_max[-1][:] if row_max else None,
+                scalar2=None,
                 op0=ALU.mult,
                 op1=ALU.max,
-                accum_out=m[:],
+                accum_out=piece_max[:, n : n + 1],
             )
-            row_max.append(m)
         neg_max = tile("neg_max", [P, 1], F32)
-        nc.vector.tensor_scalar_mul(neg_max[:], row_max[-1][:], -1.0)
+        nc.vector.tensor_reduce(neg_max[:], piece_max[:], mybir.AxisListType.X, ALU.max, negate=True)
 
 
-        v_bf = {(g, h): tile(f"v_bf{g}{h}", [P, E_HALF, PACK], BF16) for g, h in ((0, 0), (1, 0), (1, 1))}
+        v_bf = {(g, h): tile(f"v_bf{g}{h}", [P, E_HALF, PACK], BF16) for g, h in ((0, 0), (1, 0))}
         v_codes, v_scales = {}, {}
 
         def cast_values(engine, g, h, c0, c1):
@@ -159,7 +157,7 @@ def tile_attend_knockout_heads_kernel(tc, query, keys_words, keys_scales, fac, v
         nc.vector.tensor_copy(pf[:].indirect(offsets[:]), pk[:])
         z = tile("z", [P, 1], F32)
         nc.scalar.activation(p[:], a_sb[:], ACT.Exp, bias=neg_max[:], accum_out=z[:])
-        for g, h in ((0, 1), (1, 0), (1, 1)):
+        for g, h in ((0, 1), (1, 0)):
             cast_values("scalar", g, h, 0, 128)
             cast_values("scalar", g, h, 128, 256)
         inv_z = tile("inv_z", [P, 1], F32)
@@ -184,6 +182,9 @@ def tile_attend_knockout_heads_kernel(tc, query, keys_words, keys_scales, fac, v
         for g in range(PASSES):
             cols = slice(g * K_PASS, (g + 1) * K_PASS)
             nc.vector.scalar_tensor_tensor(out=u[g][:], in0=p[:, cols], scalar=share[:], in1=pf[:, cols], op0=ALU.mult, op1=ALU.subtract)
+        v_bf[1, 1] = tile("v_bf11", [P, E_HALF, PACK], BF16, tag="p")
+        cast_values("gpsimd", 1, 1, 0, 128)
+        cast_values("gpsimd", 1, 1, 128, 256)
         w_bf = []
         for g in range(PASSES):
             cols = slice(g * K_PASS, (g + 1) * K_PASS)
@@ -218,9 +219,9 @@ def tile_attend_knockout_heads_kernel(tc, query, keys_words, keys_scales, fac, v
 
         turn(0)
         turn(1)
-        quantize_values(0, 1, tag="p")
-        quantize_values(1, 0, tag="u0")
+        quantize_values(0, 1, tag="u0")
         quantize_weights(0)
+        quantize_values(1, 0, tag="u1")
         quantize_values(1, 1)
         quantize_weights(1)
 

@@ -117,7 +117,7 @@ def tile_attend_knockout_heads_kernel(tc, query, keys_words, keys_scales, fac, v
         nc.vector.tensor_reduce(neg_max[:], piece_max[:], mybir.AxisListType.X, ALU.max, negate=True)
 
 
-        v_bf = {(g, h): tile(f"v_bf{g}{h}", [P, E_HALF, PACK], BF16) for g, h in ((0, 0), (1, 0))}
+        v_bf = {(g, h): tile(f"v_bf{g}{h}", [P, E_HALF, PACK], BF16) for g, h in ((0, 0), (1, 0), (1, 1))}
         v_codes, v_scales = {}, {}
 
         def cast_values(engine, g, h, c0, c1):
@@ -157,7 +157,7 @@ def tile_attend_knockout_heads_kernel(tc, query, keys_words, keys_scales, fac, v
         nc.vector.tensor_copy(pf[:].indirect(offsets[:]), pk[:])
         z = tile("z", [P, 1], F32)
         nc.scalar.activation(p[:], a_sb[:], ACT.Exp, bias=neg_max[:], accum_out=z[:])
-        for g, h in ((0, 1), (1, 0)):
+        for g, h in ((0, 1), (1, 0), (1, 1)):
             cast_values("scalar", g, h, 0, 128)
             cast_values("scalar", g, h, 128, 256)
         inv_z = tile("inv_z", [P, 1], F32)
@@ -182,31 +182,27 @@ def tile_attend_knockout_heads_kernel(tc, query, keys_words, keys_scales, fac, v
         for g in range(PASSES):
             cols = slice(g * K_PASS, (g + 1) * K_PASS)
             nc.vector.scalar_tensor_tensor(out=u[g][:], in0=p[:, cols], scalar=share[:], in1=pf[:, cols], op0=ALU.mult, op1=ALU.subtract)
-        v_bf[1, 1] = tile("v_bf11", [P, E_HALF, PACK], BF16, tag="p")
-        cast_values("gpsimd", 1, 1, 0, 128)
-        cast_values("gpsimd", 1, 1, 128, 256)
-        w_bf = []
+        w_bf = {}
         for g in range(PASSES):
-            cols = slice(g * K_PASS, (g + 1) * K_PASS)
-            w = tile(f"w_bf{g}", [P, K_PASS], BF16)
-            nc.vector.scalar_tensor_tensor(
-                out=w[:].rearrange("q (k r) -> q k r", r=PACK),
-                in0=u[g][:].rearrange("q (k r) -> q k r", r=PACK),
-                scalar=neg_inv_z2[:],
-                in1=fac_ps[g][:].rearrange("q r k -> q k r"),
-                op0=ALU.mult,
-                op1=ALU.mult,
-            )
-            w_bf.append(w)
+            for s in range(2):
+                w = tile(f"w_bf{g}{s}", [P, P, 2], BF16)
+                nc.vector.scalar_tensor_tensor(
+                    out=w[:],
+                    in0=u[g][:].rearrange("q (k r) -> q k r", r=PACK)[:, :, 2 * s : 2 * s + 2],
+                    scalar=neg_inv_z2[:],
+                    in1=fac_ps[g][:, 2 * s : 2 * s + 2, :].rearrange("q r k -> q k r"),
+                    op0=ALU.mult,
+                    op1=ALU.mult,
+                )
+                w_bf[g, s] = w
 
 
         wt_bf = []
 
         def turn(g):
-            words = w_bf[g][:].bitcast(F32)
             turned = ps.tile([P, 2, Q], F32, name=f"turned{g}")
             for s in range(2):
-                nc.tensor.transpose(turned[:, s, :], words[:, s : 2 * P : 2], ident[:])
+                nc.tensor.transpose(turned[:, s, :], w_bf[g, s][:].rearrange("q k e -> q (k e)").bitcast(F32), ident[:])
             wt = tile(f"wt_bf{g}", [P, Q * PACK], BF16)
             nc.scalar.copy(out=wt[:].bitcast(F32).rearrange("p (q s) -> p q s", s=2), in_=turned[:].rearrange("p s q -> p q s"))
             wt_bf.append(wt)
@@ -219,9 +215,9 @@ def tile_attend_knockout_heads_kernel(tc, query, keys_words, keys_scales, fac, v
 
         turn(0)
         turn(1)
-        quantize_values(0, 1, tag="u0")
+        quantize_values(0, 1, tag="p")
+        quantize_values(1, 0, tag="u0")
         quantize_weights(0)
-        quantize_values(1, 0, tag="u1")
         quantize_values(1, 1)
         quantize_weights(1)
 

from contextlib import ExitStack

import concourse.mybir as mybir
from concourse.masks import make_identity

D, T, Q, I, E = 512, 1024, 128, 256, 512
FLOPS = 2 * Q * D * T + 2 * Q * T * E

F32 = mybir.dt.float32
BF16 = mybir.dt.bfloat16
I32 = mybir.dt.int32
U32 = mybir.dt.uint32
U16 = mybir.dt.uint16
U8 = mybir.dt.uint8
FP8X4 = mybir.dt.float8_e4m3fn_x4
ALU = mybir.AluOpType
ACT = mybir.ActivationFunctionType

P = 128
PACK = 4
K_PASS = P * PACK
PASSES = T // K_PASS
BANK = 512
E_HALF = E // 2


def tile_attend_knockout_heads_kernel(tc, query, keys_words, keys_scales, fac, vals, offs, out):
    nc = tc.nc
    with ExitStack() as ctx:
        sb = ctx.enter_context(tc.tile_pool(name="sb", bufs=1))
        ps = ctx.enter_context(tc.psum_pool(name="ps", bufs=1))

        def tile(name, shape, dtype, tag=""):
            return sb.tile(shape, dtype, name=name, tag=tag, align_bytes=64)

        k_scales = tile("k_scales", [P, BANK], U8)
        nc.gpsimd.memset(k_scales[:].bitcast(U32), 0)
        q_raw = tile("q_raw", [P, PACK, Q], F32)
        nc.sync.dma_start(out=q_raw[:], in_=query.rearrange("(p j) q -> p j q", j=PACK))
        for quad in range(4):
            nc.sync.dma_start(
                out=k_scales[32 * quad : 32 * quad + 8, :].bitcast(I32),
                in_=keys_scales[0][4 * quad : 4 * quad + 4, :].bitcast(I32).rearrange("r (h c) -> h r c", h=2),
            )
        k_bytes = keys_words[0].rearrange("p n t -> p (n t)")
        rows = [vals[g * K_PASS : (g + 1) * K_PASS, :].rearrange("(p j) e -> p j e", j=PACK) for g in range(PASSES)]
        v_raw = {}

        def load_values(g, c0, c1):
            vr = tile(f"v_raw{g}_{c0}", [P, PACK, c1 - c0], F32)
            nc.sync.dma_start(out=vr[:], in_=rows[g][:, :, c0:c1])
            for c in range(c0, c1, P):
                v_raw[g, c] = vr[:, :, c - c0 : c - c0 + P]

        k_words = []

        def load_keys(h):
            kw = tile(f"k_words{h}", [P, BANK], U32)
            nc.sync.dma_start(out=kw[:].bitcast(I32), in_=k_bytes[:, h * BANK * PACK : (h + 1) * BANK * PACK].bitcast(I32))
            k_words.append(kw)

        offsets = sb.tile([P, I // 16], U16, name="offsets")
        load_keys(0)
        load_keys(1)
        load_values(0, 0, 256)
        nc.sync.dma_start(offsets[:], offs)
        load_values(0, 256, 512)
        load_values(1, 0, 512)
        fac_sb = tile("fac_sb", [P, PASSES, PACK], F32)
        nc.gpsimd.dma_start(out=fac_sb[:], in_=fac[0].rearrange("(g p r) -> p g r", g=PASSES, r=PACK))

        ident = tile("ident", [P, P], F32)
        make_identity(nc, ident[:])
        pf = tile("pf", [P, T], F32)
        nc.vector.memset(pf[:], 0.0)
        warm = tile("warm", [P, 1], F32)
        nc.vector.memset(warm[:], 0.0)
        warm_out = tile("warm_out", [P, 1], F32)
        nc.scalar.activation(warm_out[:], warm[:], ACT.Exp)

        q_bf = [tile(f"q_bf{h}", [P, Q // 2, PACK], BF16) for h in range(2)]
        q_codes = tile("q_codes", [P, Q], U32)
        q_scales = tile("q_scales", [P, Q], U8)
        for h in range(2):
            nc.vector.tensor_copy(
                out=q_bf[h][:].rearrange("p (c i) t -> p c t i", i=4),
                in_=q_raw[:, :, h * 64 : (h + 1) * 64].rearrange("p t (c i) -> p c t i", i=4),
            )
        for h in range(2):
            cols = slice(h * 64, (h + 1) * 64)
            nc.vector.quantize_mx(out=q_codes[:, cols].bitcast(FP8X4), scales=q_scales[:, cols], in_=q_bf[h][:].rearrange("p q j -> p (q j)"))


        a_sb = tile("a_sb", [P, T], F32)
        piece_max = tile("piece_max", [P, 3], F32)
        for n, (h, c0, c1) in enumerate(((0, 0, 256), (0, 256, 512), (1, 0, 512))):
            a_ps = ps.tile([P, c1 - c0], F32, name=f"a_ps{h}_{c0}", tag=f"ab{h}" if c1 == BANK else "a_first")
            nc.tensor.matmul_mx(
                out=a_ps[:],
                lhsT=q_codes[:].bitcast(FP8X4),
                lhsT_scale=q_scales[:],
                rhs=k_words[h][:, c0:c1].bitcast(FP8X4),
                rhs_scale=k_scales[4 * h :, c0:c1],
                start=True,
                stop=True,
            )
            nc.vector.tensor_scalar(
                out=a_sb[:, h * BANK + c0 : h * BANK + c1],
                in0=a_ps[:],
                scalar1=1.0,
                scalar2=None,
                op0=ALU.mult,
                op1=ALU.max,
                accum_out=piece_max[:, n : n + 1],
            )
        neg_max = tile("neg_max", [P, 1], F32)
        nc.vector.tensor_reduce(neg_max[:], piece_max[:], mybir.AxisListType.X, ALU.max, negate=True)


        v_bf = {(g, h): tile(f"v_bf{g}{h}", [P, E_HALF, PACK], BF16) for g, h in ((0, 0), (1, 0), (1, 1))}
        v_codes, v_scales = {}, {}

        def cast_values(engine, g, h, c0, c1):
            cols = slice(c0, c1)
            dst, src = v_bf[g, h][:, cols, :], v_raw[g, h * E_HALF + c0]
            if engine == "gpsimd":
                nc.gpsimd.tensor_scalar(out=dst, in0=src.rearrange("p t c -> p c t"), scalar1=1.0, scalar2=0.0, op0=ALU.mult, op1=ALU.add)
                return
            dst = dst.rearrange("p (c i) t -> p c t i", i=4)
            src = src.rearrange("p t (c i) -> p c t i", i=4)
            if engine == "scalar":
                nc.scalar.copy(out=dst, in_=src)
            else:
                nc.vector.tensor_copy(out=dst, in_=src)

        def quantize_values(g, h, tag=""):
            v_codes[g, h] = tile(f"v_codes{g}{h}", [P, E_HALF], U32, tag=tag)
            v_scales[g, h] = tile(f"v_scales{g}{h}", [P, E_HALF], U8)
            nc.vector.quantize_mx(
                out=v_codes[g, h][:].bitcast(FP8X4),
                scales=v_scales[g, h][:],
                in_=v_bf[g, h][:].rearrange("p e j -> p (e j)"),
            )

        cast_values("scalar", 0, 0, 0, 128)
        cast_values("scalar", 0, 0, 128, 256)

        a_listed = tile("a_listed", [P, I], F32, tag="listed")
        nc.vector.tensor_copy(a_listed[:], a_sb[:].indirect(offsets[:]))
        p = tile("p", [P, T], F32, tag="p")
        pk = tile("pk", [P, I], F32)
        sum_k = tile("sum_k", [P, 1], F32)
        nc.scalar.activation(pk[:], a_listed[:], ACT.Exp, bias=neg_max[:], accum_out=sum_k[:])

        quantize_values(0, 0)
        v_bf[0, 1] = tile("v_bf01", [P, E_HALF, PACK], BF16, tag="listed")
        nc.vector.tensor_copy(pf[:].indirect(offsets[:]), pk[:])
        z = tile("z", [P, 1], F32)
        nc.scalar.activation(p[:], a_sb[:], ACT.Exp, bias=neg_max[:], accum_out=z[:])
        for g, h in ((0, 1), (1, 0), (1, 1)):
            cast_values("scalar", g, h, 0, 128)
            cast_values("scalar", g, h, 128, 256)
        inv_z = tile("inv_z", [P, 1], F32)
        nc.vector.reciprocal(inv_z[:], z[:])
        neg_z2 = tile("neg_z2", [P, 1], F32)
        nc.vector.tensor_sub(neg_z2[:], sum_k[:], z[:])

        share = tile("share", [P, 1], F32)
        nc.vector.tensor_mul(share[:], sum_k[:], inv_z[:])
        neg_inv_z2 = tile("neg_inv_z2", [P, 1], F32)
        nc.vector.reciprocal(neg_inv_z2[:], neg_z2[:])


        fac_ps = []
        for g in range(PASSES):
            f = ps.tile([P, PACK, P], F32, name=f"fac_ps{g}", tag=f"ab{g}")
            for r in range(PACK):
                nc.tensor.transpose(f[:, r, :], fac_sb[:, g, r : r + 1].to_broadcast([P, P]), ident[:])
            fac_ps.append(f)

        u = [tile(f"u{g}", [P, K_PASS], F32, tag=f"u{g}") for g in range(PASSES)]
        for g in range(PASSES):
            cols = slice(g * K_PASS, (g + 1) * K_PASS)
            nc.vector.scalar_tensor_tensor(out=u[g][:], in0=p[:, cols], scalar=share[:], in1=pf[:, cols], op0=ALU.mult, op1=ALU.subtract)
        w_bf = {}
        for g in range(PASSES):
            for s in range(2):
                w = tile(f"w_bf{g}{s}", [P, P, 2], BF16)
                nc.vector.scalar_tensor_tensor(
                    out=w[:],
                    in0=u[g][:].rearrange("q (k r) -> q k r", r=PACK)[:, :, 2 * s : 2 * s + 2],
                    scalar=neg_inv_z2[:],
                    in1=fac_ps[g][:, 2 * s : 2 * s + 2, :].rearrange("q r k -> q k r"),
                    op0=ALU.mult,
                    op1=ALU.mult,
                )
                w_bf[g, s] = w


        wt_bf = []

        def turn(g):
            turned = ps.tile([P, 2, Q], F32, name=f"turned{g}")
            for s in range(2):
                nc.tensor.transpose(turned[:, s, :], w_bf[g, s][:].rearrange("q k e -> q (k e)").bitcast(F32), ident[:])
            wt = tile(f"wt_bf{g}", [P, Q * PACK], BF16)
            nc.scalar.copy(out=wt[:].bitcast(F32).rearrange("p (q s) -> p q s", s=2), in_=turned[:].rearrange("p s q -> p q s"))
            wt_bf.append(wt)

        w_codes = [tile(f"w_codes{g}", [P, Q], U32) for g in range(PASSES)]
        w_scales = [tile(f"w_scales{g}", [P, Q], U8) for g in range(PASSES)]

        def quantize_weights(g):
            nc.vector.quantize_mx(out=w_codes[g][:].bitcast(FP8X4), scales=w_scales[g][:], in_=wt_bf[g][:])

        turn(0)
        turn(1)
        quantize_values(0, 1, tag="p")
        quantize_values(1, 0, tag="u0")
        quantize_weights(0)
        quantize_values(1, 1)
        quantize_weights(1)

        o_ps = [ps.tile([P, E_HALF], F32, name=f"o_ps{h}") for h in range(2)]
        for g in range(PASSES):
            for h in range(2):
                cols = slice(h * E_HALF, (h + 1) * E_HALF)
                nc.tensor.matmul_mx(
                    out=o_ps[h][:],
                    lhsT=w_codes[g][:].bitcast(FP8X4),
                    lhsT_scale=w_scales[g][:],
                    rhs=v_codes[g, h][:].bitcast(FP8X4),
                    rhs_scale=v_scales[g, h][:],
                    start=(g == 0),
                    stop=(g == PASSES - 1),
                )
        for h in range(2):
            cols = slice(h * E_HALF, (h + 1) * E_HALF)
            o_sb = tile(f"o_sb{h}", [P, E_HALF], F32)
            if h == 0:
                nc.vector.tensor_copy(out=o_sb[:], in_=o_ps[h][:])
                nc.sync.dma_start(out=out[:, cols], in_=o_sb[:])
            else:
                nc.scalar.copy(out=o_sb[:], in_=o_ps[h][:])
                nc.scalar.dma_start(out=out[:, cols], in_=o_sb[:])
